import numpy as np, ml_dtypes
CORES = [10,34,74,98]
N = 4
BF = ml_dtypes.bfloat16
def gentries(a):
    return np.ascontiguousarray(a.reshape(8, 16, -1).transpose(0, 2, 1)).reshape(8, -1)
def gtable(e):
    e = np.asarray(e); return np.ascontiguousarray(e.reshape(8, -1, 16).transpose(0, 2, 1)).reshape(128, -1).astype(np.int32)
L, E, H, RO = 3, 512, 1, 2
V = L * E; W = (1 + H) * V
def feed(rng, far, void):
    x = rng.integers(V, W, (N, 8, 16, V))
    for l in range(1, L):
        s = slice(l * E, (l + 1) * E); own = rng.integers(0, l * E, (N, 8, 16, E))
        x[..., s] = np.where(rng.random(own.shape) < far, x[..., s], own)
    return np.where(rng.random(x.shape) < void, -1, x)
def edges(rng):
    x = np.zeros((N, 8, 16, V), np.int64)
    for l in range(L):
        few = np.array(([0, l * E - 1, V, W - 1] if l else [V, 2 * V - 1, W - 1]) + ([2 * V, H * V] if H > 1 else []))
        x[..., l * E:(l + 1) * E] = rng.choice(few, (N, 8, 16, E))
    return x
def links(rng):
    return np.argsort(rng.random((N, 8, L, E)), axis=-1).reshape(N, 8, V)
def first(rng, empty):
    cf = rng.integers(V, W, (N, 8, E))
    return np.where(rng.random(cf.shape) < empty, -1, cf), rng.integers(0, 17, (N, 8, E))
def near(rng, base):
    return np.clip(base + rng.integers(-20, 21, (N, 8, 16, V)), 0, 255)
def pack(fd, pw, bs, dl, nx, t0, cf, cw):
    def lanes(a): return np.ascontiguousarray(a.reshape(N, 128, V)).astype(np.float32).astype(BF)
    return {"fd": np.ascontiguousarray(fd.reshape(N, 128, V)).astype(np.int32), "pw": lanes(pw), "bs": lanes(bs), "t0": lanes(t0),
            "dl": dl.astype(np.int32), "nx": np.stack([gtable(a) for a in nx]), "cf": cf.astype(np.int32), "cw": cw.astype(np.int32)}
def setup_inputs(rng):
    base = rng.integers(0, 236, (N, 8, 1, V)); void = rng.choice(np.array([0.0, 0.05, 0.2, 0.7]), (N, 8, 1, V))
    pw = np.minimum((17 * rng.random((N, 8, 16, V)) ** 2).astype(np.int64), 16)
    pw = np.where(rng.random((N, 8, 1, V)) < 0.125, pw[:, :, :1], pw)
    cf, cw = first(rng, 0.25)
    return pack(feed(rng, 0.4, void), pw, near(rng, base), rng.integers(1, 5, (N, 8, V)), links(rng), near(rng, base), cf, cw)
def setup_inputs_spread(rng):
    bs = np.minimum((np.exp2(8 * rng.random((N, 8, 1, V))) * rng.random((N, 8, 16, V))).astype(np.int64), 255)
    t0 = np.minimum((np.exp2(8 * rng.random((N, 8, 1, V))) * rng.random((N, 8, 16, V))).astype(np.int64), 255)
    bs = np.where(rng.random(bs.shape) < 0.02, 255, bs); t0 = np.where(rng.random(t0.shape) < 0.02, 255, t0)
    pw = np.minimum((17 * rng.random((N, 8, 16, V)) ** rng.choice(np.array([0.5, 1.0, 3.0, 8.0]), (N, 8, 1, V))).astype(np.int64), 16)
    x = feed(rng, rng.choice(np.array([0.05, 0.5, 0.95]), (N, 8, 1, 1)), rng.random((N, 8, 1, V)) ** 2)
    crowd = V + ((x - V) * rng.random(x.shape) ** 3).astype(np.int64)
    x = np.where((x >= V) & (np.arange(8)[None, :, None, None] % 2 == 1), crowd, x)
    cf, cw = first(rng, 0.4)
    return pack(x, pw, bs, rng.choice(np.array([1, 1, 1, 2, 3, 4]), (N, 8, V)), links(rng), t0, cf, cw)
def setup_inputs_ends(rng):
    def two():
        m = rng.choice(np.array([0, 1, 2]), (N, 8, 1, V), p=[0.45, 0.2, 0.35])
        return 255 * np.where(m == 2, rng.integers(0, 2, (N, 8, 16, V)), m)
    bs = two(); t0 = two()
    pw = 16 * (rng.random((N, 8, 16, V)) < rng.choice(np.array([0.0, 0.06, 1.0]), (N, 8, 1, V), p=[0.6, 0.3, 0.1])).astype(np.int64)
    u = rng.random((N, 8, 16, V)); x = np.where(u < 0.35, -1, np.where(u < 0.75, W - 1, edges(rng)))
    bs[N - 1, 7, :, V - 1] = 255; t0[N - 1, 7, :, V - 1] = 255; pw[N - 1, 7, :, V - 1] = 0
    t0[N - 1 - H, 7 - H, :, V - 1] = 255; bs[N - 1, 7, :, E - 1] = 0; t0[N - 1, 7, :, E - 1] = 0; pw[N - 1, 7, :, E - 1] = 0; x[N - 1, 7, :, E - 1] = W - 1
    mid = 1 + np.argsort(rng.random((N, 8, L, E - 2)), axis=-1); one = np.ones((N, 8, L, 1), np.int64)
    nx = np.where(rng.random((N, 8, L, 1)) < 0.5, np.arange(E)[::-1], np.concatenate([(E - 1) * one, mid, 0 * one], axis=-1))
    c = rng.random((N, 8, E)); cf = np.where(c < 0.45, -1, np.where(c < 0.85, W - 1, V)); cf[N - 1, 7, E - 1] = W - 1
    return pack(x, pw, bs, 1 + 3 * rng.integers(0, 2, (N, 8, V)), nx.reshape(N, 8, V), t0, cf, 16 * rng.integers(0, 2, (N, 8, E)))
def setup_inputs_corners(rng):
    kd = np.argsort(rng.random((N, 8)), axis=1)[:, :, None, None]; ke = kd[..., 0]
    base = rng.integers(0, 236, (N, 8, 1, V)); bs = near(rng, base); t0 = near(rng, base); e = rng.random((N, 8, 1, V))
    bs = np.where(e < 0.1, 0, np.where(e < 0.15, 255, bs)); t0 = np.where(e < 0.05, 0, np.where((e > 0.12) & (e < 0.2), 255, t0))
    nv = rng.choice(np.array([0, 1, 15, 16]), (N, 8, 1, V))
    for k, n in ((0, 0), (1, 16), (2, 0), (3, 1), (4, 15)): nv = np.where(kd == k, n, nv)
    x = np.where(kd == 5, edges(rng), feed(rng, 0.5, 0.0))
    x = np.where(np.argsort(rng.random((N, 8, 16, V)), axis=2) < nv, -1, x)
    pw = rng.integers(0, 17, (N, 8, 16, V))
    pw = np.where(kd == 3, pw[:, :, :1], np.where(kd == 5, 16 * rng.integers(0, 2, pw.shape), np.where(kd == 0, 16, np.where(kd == 2, 0, pw))))
    cf, cw = first(rng, 0.3); full, heavy = first(rng, 0.0)
    cf = np.where(ke == 1, -1, np.where((ke == 0) | (ke == 2) | (ke == 4), full, cf))
    cw = np.where(ke == 0, rng.choice(np.array([0, 15, 16]), cw.shape), np.where(ke == 2, 0, np.where(ke == 4, 16, cw)))
    return pack(x, pw, bs, rng.integers(1, 5, (N, 8, V)), links(rng), t0, cf, cw)
def setup_inputs_heavy(rng):
    late = np.arange(V) >= E
    bs = rng.integers(0, 201, (N, 8, 16, V)); t0 = rng.integers(1, 151, (N, 8, 16, V))
    low = late & (rng.random((N, 8, 1, V)) < 0.4); bs = np.where(low, 0, bs); t0 = np.where(low, 0, t0)
    n15 = rng.choice(np.array([0, 0, 1, 1, 2, 16]), (N, 8, 1, V))
    pw = np.where(np.argsort(rng.random((N, 8, 16, V)), axis=2) < n15, 15, 16)
    light = late & (rng.random((N, 8, 1, V)) < 0.75); pw = np.where(light, rng.integers(0, 15, pw.shape), pw)
    x = feed(rng, 0.5, np.where(light, 0.2, 0.0))
    cf, cw = first(rng, 0.1); cw = rng.choice(np.array([16, 16, 16, 15]), cw.shape)
    return pack(x, pw, bs, rng.integers(1, 5, (N, 8, V)), links(rng), t0, cf, cw)
def setup_inputs_ties(rng):
    lv = 3 * np.repeat(np.arange(L), E)
    bs = 60 + lv + rng.integers(0, 4, (N, 8, 16, V)); t0 = 60 + lv + rng.integers(0, 4, (N, 8, 16, V))
    lift = (rng.random((N, 8, 16, V)) < 0.3) & (rng.random((N, 8, 1, V)) < 0.5)
    pw = rng.choice(np.array([4, 8, 8, 9, 12, 15]), (N, 8, 1, V)) + lift.astype(np.int64)
    x = feed(rng, 0.5, rng.choice(np.array([0.0, 0.0, 0.1]), (N, 8, 1, V)))
    cf, cw = first(rng, 0.1); cw = rng.choice(np.array([4, 8, 9, 12]), cw.shape)
    return pack(x, pw, bs, 1 + 3 * (rng.random((N, 8, V)) < 0.2).astype(np.int64), links(rng), t0, cf, cw)
def check_inputs(d):
    bad = []
    for k, lo, hi in (("fd", -1, W - 1), ("pw", 0, 16), ("bs", 0, 255), ("t0", 0, 255), ("dl", 1, 4), ("nx", 0, E - 1), ("cf", -1, W - 1), ("cw", 0, 16)):
        a = np.asarray(d[k]).astype(np.float64)
        if not (np.all(a >= lo) and np.all(a <= hi) and np.all(a == np.floor(a))): bad.append("range of " + k)
    x = d["fd"].reshape(N, 128, L, E); c = d["cf"]
    if np.any((x < V) & (x >= (np.arange(L) * E)[None, None, :, None])): bad.append("own feeders of fd lie in earlier levels")
    if np.any((c >= 0) & (c < V)): bad.append("first carried feeders of cf are foreign")
    n = np.stack([gentries(a) for a in d["nx"]]).reshape(N, 8, L, E)
    if np.any(np.sort(n, axis=-1) != np.arange(E)): bad.append("nx is a permutation in each level")
    return bad
def reference(fd, pw, bs, t0, dl, nx, cf, cw):
    fe = fd.astype(np.int64).reshape(N, 8, 16, V); wt = np.where(fe < 0, -1, pw.astype(np.float32).astype(np.int64).reshape(N, 8, 16, V))
    base = bs.astype(np.float32).astype(np.int32).reshape(N, 8, 16, V); T = t0.astype(np.float32).astype(np.int32).reshape(N, 8, 16, V)
    to = np.stack([gentries(a) for a in nx]).astype(np.int64); dd = dl.astype(np.int32)[:, :, None, :]
    inf = cf.astype(np.int64); inw = np.where(inf < 0, -1, cw.astype(np.int64))
    rows = np.arange(16)[None, None, :, None]
    for q in range(RO):
        old = T.copy()
        win = np.concatenate([T] + [np.roll(old, (h, h), (0, 1)) for h in range(1, H + 1)], axis=3)
        for l in range(L):
            s = slice(l * E, (l + 1) * E); f = fe[..., s]; w = wt[..., s]
            m = np.argmin(w, axis=2)[:, :, None]
            lf = np.take_along_axis(f, m, 2)[:, :, 0]; lw = np.take_along_axis(w, m, 2)[:, :, 0]
            enter = inw > lw; put = enter[:, :, None] & (rows == m)
            hf = np.where(enter, lf, inf); hw = np.where(enter, lw, inw)
            f = np.where(put, inf[:, :, None], f); w = np.where(put, inw[:, :, None], w)
            b = (base[..., s] + old[..., s]) >> 1
            a = np.take_along_axis(win, np.maximum(f, 0).reshape(N, 8, 1, 16 * E), 3).reshape(N, 8, 16, 16, E)
            c = np.add.reduce(a > b[:, :, :, None], axis=2, dtype=np.int64)
            drop = c > w
            t = np.max(np.where(drop[:, :, None], 0, a), axis=3)
            T[..., s] = np.minimum(255, np.maximum(b, t) + dd[..., s]); win[..., s] = T[..., s]
            v = np.where(drop, w, -1); m = np.argmax(v, axis=2)[:, :, None]
            gf = np.take_along_axis(f, m, 2)[:, :, 0]; gw = np.take_along_axis(v, m, 2)[:, :, 0]
            take = gw > hw; gone = take[:, :, None] & (rows == m)
            outf = np.where(take, gf, hf); outw = np.where(take, gw, hw)
            fe[..., s] = np.where(gone, -1, f); wt[..., s] = np.where(gone, -1, w)
            if l == L - 1: outf = np.where(outw < 0, -1, V + l * E + np.arange(E))
            inf = np.zeros_like(outf); inw = np.zeros_like(outw)
            np.put_along_axis(inf, to[..., s], outf, 2); np.put_along_axis(inw, to[..., s], outw, 2)
            if l == L - 1: inf = np.roll(inf, (1, 1), (0, 1)); inw = np.roll(inw, (1, 1), (0, 1))
    return {"yt": np.ascontiguousarray(T.reshape(N, 128, V)).astype(np.float32).astype(BF)}

import math
from concourse.mybir import dt, AluOpType, AxisListType, ActivationFunctionType

ALU = AluOpType
ACT = ActivationFunctionType
K = 32768.0
BASE = 40.0
DIAG = 25.0
EA = math.log(BASE) / K
C_UP = 20 * math.log(2.0)
C_DN = 17.1 * math.log(BASE) + C_UP
CY = 0.83 * 1.2
PCY = 0.5
GTH = 1.56
GSTEP = 1
CHUNKS = (2, 2)
SETUP = (0, 0, 0, 1, 1, 1)
OVH = 40.0
POVH = 15.0
SLACK = 0.3
REPDMA = 0
HPE = 0
TRIES = 6
RUSH = 4
PASSES = 6
ROUNDS = 1500
ORDER = []
HOP = 100.0

SCRATCH = {}


def _sb(name, cols, dtype):
    SCRATCH[name] = ("sbuf", [128, cols], dtype)


for _n, _c, _d in (
        ("fdn", 1536, "int32"), ("pwn", 1536, "bfloat16"), ("bsn", 1536, "bfloat16"), ("t0n", 1536, "bfloat16"),
        ("nxn", 96, "int32"), ("nxu", 96, "uint16"), ("dln", 256, "int32"), ("dlb", 256, "bfloat16"), ("seld", 768, "bfloat16"),
        ("cfn", 256, "int32"), ("cwn", 256, "int32"), ("cfh", 256, "float16"), ("cwb", 256, "bfloat16"), ("cvb", 256, "bfloat16"),
        ("fdh", 1536, "float16"), ("fvb", 1536, "bfloat16"),
        ("tsend", 1536, "bfloat16"), ("tland", 1536, "bfloat16"), ("landt", 1536, "bfloat16"),
        ("invn", 1536, "bfloat16"), ("invc", 96, "bfloat16"), ("invu", 96, "uint16"),
        ("iov", 512, "bfloat16"), ("ioe", 512, "float32"), ("bsum", 512, "float32"), ("inf", 128, "float32"), ("outi", 512, "int32"), ("outj", 512, "int32"), ("ioi", 16, "int32"), ("ioj", 16, "int32"), ("oneh", 16, "float32"),
        ("ones", 256, "bfloat16"), ("c256", 128, "bfloat16"), ("bo", 128, "bfloat16"), ("bot", 128, "bfloat16"), ("bof", 128, "float32"),
        ("ident", 128, "bfloat16"), ("ihalf", 128, "bfloat16"), ("ineg", 128, "bfloat16"), ("i256", 128, "bfloat16"), ("im256", 128, "bfloat16"),
        ("mlo", 128, "bfloat16"), ("mhi", 128, "bfloat16"), ("mm1", 128, "bfloat16"), ("mm2", 128, "bfloat16"), ("mm3", 128, "bfloat16"), ("mwin", 128, "bfloat16"),
        ("sel", 512, "bfloat16"), ("selk", 512, "bfloat16"), ("selh", 512, "bfloat16"), ("self", 512, "float16"), ("selr", 256, "bfloat16"),
        ("sel8", 256, "bfloat16"), ("sel8k", 256, "bfloat16"), ("sel8f", 256, "float16"),
        ("lk", 2048, "bfloat16"), ("sk", 2048, "bfloat16"), ("ramp", 256, "bfloat16"),
        ("qs", 1536, "float32"), ("dr", 1536, "float32"), ("tt", 3072, "bfloat16"),
        ("mbs", 1024, "float32"), ("insend", 512, "float32"), ("inland", 512, "float32")):
    _sb(_n, _c, _d)
for _s in range(2):
    for _n, _c, _d in (
            ("wina", 3072, "bfloat16"), ("winb", 3072, "bfloat16"), ("aa", 4096, "bfloat16"), ("gg", 4096, "bfloat16"),
            ("rr", 2048, "float32"), ("inn", 256, "float32"), ("edn", 256, "bfloat16"), ("ein", 256, "bfloat16"),
            ("dlt", 256, "float32"), ("qi", 256, "int32"), ("fi", 256, "int32"), ("off", 256, "uint16"),
            ("eup", 256, "float32"), ("hh", 256, "float32"), ("eh", 256, "bfloat16"), ("ed", 256, "bfloat16"),
            ("yy", 256, "bfloat16"), ("gq", 256, "float32"), ("hrep", 512, "float32"),
            ("rep", 512, "float32"), ("vi", 256, "int32")):
        _sb(_n + str(_s), _c, _d)
for _n in ("pma0", "pma1", "pmb", "ph0", "ph1", "pcn", "px0", "px1"):
    SCRATCH[_n] = ("psum", [128, 512], "float32")

NDMA = 90
SEMAPHORES = ["eV", "eS", "eP", "eG", "sent"] + ["d%d" % _i for _i in range(NDMA)] + ["r%d" % _i for _i in range(10)]


def build_graph(g, T, topo, core):
    ops, lastw, readers, bank, stage, nlev = [], {}, {}, {}, [-3.0], [0]
    V, S, P = g.vector, g.scalar, g.tensor
    rank = T.rank_of(core)
    nxt = T.cores[(rank + 1) % len(T.cores)]
    rid, pid = topo.addr(nxt)[0], topo.addr(nxt)[1]
    mask = topo.mask(core, nxt)
    neng = len(topo.engines(core, nxt))

    def op(eng, fn, cost, r=(), w=(), b=(), lat=0.0, kind="c", sem=None, after=None):
        me = len(ops)
        deps = set()
        for k in r:
            if k in lastw:
                deps.add(lastw[k])
        for k in w:
            if k in lastw:
                deps.add(lastw[k])
            deps.update(readers.get(k, ()))
        for k in r:
            readers.setdefault(k, []).append(me)
        for k in w:
            lastw[k] = me
            readers[k] = []
        for k in b:
            st = bank.setdefault(k, [None, [], []])
            if st[0] != eng:
                st[0], st[2], st[1] = eng, st[1], []
            deps.update(st[2])
            st[1].append(me)
        deps.discard(me)
        ops.append({"eng": eng, "fn": fn, "cost": cost, "deps": deps, "lat": lat, "kind": kind, "sem": sem, "after": after,
                    "w": (list(w) + [""])[0], "key": stage[0]})
        return me

    def vc(n, f=1.0):
        return OVH + max(64, n * f) * CY

    def vop(fn, n, f, r, w, b=()):
        return op("V", fn, vc(n, f), r, w, b)

    def sop(fn, n, r, w, b=()):
        return op("S", fn, 20 + vc(n), r, w, b)

    def gop(fn, n, r, w):
        return op("G", fn, 170 + 2 * n * CY, r, w)

    def mm(items, r, w, b, start=True, stop=True, apart=False):
        cost = sum(POVH + max(64, it[3]) * PCY * it[4] for it in items)

        def fn():
            ins = None
            for n, it in enumerate(items):
                ins = P.matmul(it[0], it[1], it[2], apart or (start and n == 0), apart or (stop and n == len(items) - 1))
            return ins
        return op("P", fn, cost, r, w, b)

    def dma(pairs, nbytes, r, w, q="Y", sem=None, after=None):
        return op(q, pairs, 70.0 * len(pairs), r, w, lat=2000 + nbytes / 180.0, kind="d", sem=sem, after=after)

    nrem = [0]

    def send(dst, src, nbytes, r):
        n = nrem[0]
        nrem[0] += 1
        sem = T.sem["r%d" % n]
        me = op("G", lambda: g.remote_dma(dst, src, sem, T.sem.sent, pid, rid, mask), 1000, r, (),
                lat=(6000 if n == 0 else 2500) + nbytes / 45.0, kind="r")
        return me, (sem, neng)

    arr0 = []
    for s in range(2):
        for q in range(2):
            pairs = []
            for j in range(4):
                gs = (2 * j + s - 1) % 8
                pairs.append((T.tsend[64 * q + 16 * j:64 * q + 16 * j + 16, 768 * s:768 * s + 768],
                              T.t0[16 * gs:16 * gs + 16, 768 * q:768 * q + 768]))
            dma(pairs, 98304, (), ["tsend%d%d" % (s, q)], q="Y" if q == 0 or s == 1 else "S")
        arr0.append(send(T.tland[:, 768 * s:768 * s + 768], T.tsend[:, 768 * s:768 * s + 768], 196608,
                         ["tsend%d0" % s, "tsend%d1" % s]))
        if s == 0:
            dma([(T.fdn[:, 0:512], T.fd[:, 0:512]), (T.pwn[:, 0:512], T.pw[:, 0:512])], 393216, (), ["fdn0", "pwn0"], q="S")
            dma([(T.cfn[0:16, :], T.cf[:, :]), (T.cwn[0:16, :], T.cw[:, :]), (T.dln[0:48, :], T.dl[:, :]),
                 (T.nxn[:, :], T.nx[:, :])], 131072, (), ["cfn", "cwn", "dln", "nxn"])
    dma([(T.bsn[:, 0:512], T.bs[:, 0:512]), (T.t0n[:, 0:512], T.t0[:, 0:512])], 262144, (), ["bsn0", "t0n0"])
    for l in (1, 2):
        c = slice(512 * l, 512 * l + 512)
        dma([(T.fdn[:, c], T.fd[:, c]), (T.pwn[:, c], T.pw[:, c]), (T.bsn[:, c], T.bs[:, c]), (T.t0n[:, c], T.t0[:, c])],
            655360, (), ["fdn%d" % l, "pwn%d" % l, "bsn%d" % l, "t0n%d" % l])
    win = [[T.wina0, T.wina1], [T.winb0, T.winb1]]
    for s in range(2):
        pairs = [(win[0][s][64 * h:64 * h + 64, 1536 + 768 * q:1536 + 768 * q + 768],
                  T.tland[64 * q:64 * q + 64, 768 * s:768 * s + 768]) for h in range(2) for q in range(2)]
        dma(pairs, 393216, (), ["wf0%d%d" % (s, l) for l in range(3)], sem=arr0[s][1], after=arr0[s][0])

    vop(lambda: V.memset(T.ones[:, :], 1.0), 256, .5, (), ["ones"])
    o128 = T.ones[:, 0:128]

    def asel(out, in_, pat, cmp, base, cm, r, w):
        gop(lambda: g.affine_select(out, in_, pat, cmp, 0.0, base, cm), 128, r, w)

    def vscale(out, in_, f, n, r, w):
        vop(lambda: V.tensor_scalar(out, in_, float(f), None, ALU.mult), n, .5, r, w)

    def scale(out, in_, f, n, r, w):
        sop(lambda: S.activation(out, in_, ACT.Identity, scale=float(f)), n, r, w)

    def sl(s, h):
        return slice(128 * (2 * s + h), 128 * (2 * s + h) + 128)

    asel(T.ident[:, :], o128, [[-1, 128]], ALU.is_equal, 0, 1, ["ones"], ["ident"])
    asel(T.bot[:, :], o128, [[-16, 8], [0, 16]], ALU.is_ge, 0, 1, ["ones"], ["bot"])
    asel(T.bo[:, :], T.bot[:, :], [[16, 8], [0, 16]], ALU.is_ge, 15, -1, ["bot"], ["bo"])
    asel(T.mlo[:, :], T.bo[:, :], [[1, 128]], ALU.is_gt, 0, -1, ["bo"], ["mlo"])
    asel(T.mhi[:, :], T.bo[:, :], [[-1, 128]], ALU.is_gt, 0, 1, ["bo"], ["mhi"])
    for s in range(2):
        for h in range(2):
            k = "%d%d" % (s, h)
            asel(T.sel[:, sl(s, h)], o128, [[-1000, 2], [-32, 4], [-1, 16]], ALU.is_equal, 1000 * h - 16 * s, 1, ["ones"], ["sel" + k])
        c = slice(256 * s, 256 * s + 256)
        c1 = slice(128 * s, 128 * s + 128)
        rs = ["sel%d0" % s, "sel%d1" % s]
        asel(T.sel8[:, c1], o128, [[-1, 2], [-4, 4], [0, 16]], ALU.is_equal, -2 * s, 1, ["ones"], ["sel8%d" % s])
        scale(T.selk[:, c], T.sel[:, c], K, 256, rs, ["selk%d" % s])
        vscale(T["self"][:, c], T.sel[:, c], 1, 256, rs, ["self%d" % s])
        scale(T.selh[:, c], T.sel[:, c], 0.5, 256, rs, ["selh%d" % s])
        scale(T.sel8k[:, c1], T.sel8[:, c1], K, 128, ["sel8%d" % s], ["sel8k%d" % s])
        vscale(T.sel8f[:, c1], T.sel8[:, c1], 1, 128, ["sel8%d" % s], ["sel8f%d" % s])
        for l in range(3):
            o = 128 * (3 * s + l)
            asel(T.seld[:, o:o + 128], o128, [[-1, 2], [-12, 4], [0, 16]], ALU.is_equal, -6 * s - 2 * l, 1, ["ones"], ["seld%d%d" % (s, l)])
    vscale(T.mm1[:, :], T.mlo[:, :], -BASE, 128, ["mlo"], ["mm1"])
    vscale(T.mm2[:, :], T.ident[:, :], DIAG, 128, ["ident"], ["mm2"])
    vop(lambda: V.tensor_tensor(T.mm3[:, :], T.mm1[:, :], T.mm2[:, :], ALU.add), 128, 2, ["mm1", "mm2"], ["mm3"])
    vop(lambda: V.tensor_tensor(T.mwin[:, :], T.mm3[:, :], T.mhi[:, :], ALU.subtract), 128, 2, ["mm3", "mhi"], ["mwin"])
    scale(T.ineg[:, :], T.ident[:, :], -BASE, 128, ["ident"], ["ineg"])
    scale(T.ihalf[:, :], T.ident[:, :], 0.5, 128, ["ident"], ["ihalf"])
    scale(T.i256[:, :], T.ident[:, :], 256, 128, ["ident"], ["i256"])
    scale(T.im256[:, :], T.ident[:, :], -256, 128, ["ident"], ["im256"])
    scale(T.bof[:, :], T.bo[:, :], 1, 128, ["bo"], ["bof"])
    if HPE:
        scale(T.inf[:, :], T.ident[:, :], -1, 128, ["ident"], ["inf"])
    vop(lambda: V.memset(T.c256[:, :], K / 128), 128, .5, (), ["c256"])
    gop(lambda: g.iota(T.ramp[:, :], [[0, 4], [2, 64]], 0, 0, allow_small_or_imprecise_dtypes=True), 256, (), ["ramp"])
    gop(lambda: g.iota(T.ioi[:, :], [[-1, 16]], 16, 1), 16, (), ["ioi"])
    gop(lambda: g.iota(T.iov[:, :], [[1, 512]], -256, 0, allow_small_or_imprecise_dtypes=True), 512, (), ["iov"])
    gop(lambda: g.iota(T.ioe[:, :], [[1, 512]], 2560, 0, allow_small_or_imprecise_dtypes=True), 512, ["tt000"], ["ioe"])
    for h in range(2):
        for hd in range(2):
            o, i0 = 128 * h + 64 * hd, 64 * h
            scale(T.bsum[:, o:o + 64], T.bo[:, i0:i0 + 64], 1, 64, ["bo"], ["bsum%d" % h])
            scale(T.bsum[:, 256 + o + 16:256 + o + 64], T.bo[:, i0:i0 + 48], 1, 48, ["bo"], ["bsum%d" % (2 + h)])
            scale(T.bsum[:, 256 + o:256 + o + 16], T.bo[:, i0 + 48:i0 + 64], 1, 16, ["bo"], ["bsum%d" % (2 + h)])
    vop(lambda: V.tensor_scalar(T.ioj[:, :], T.ioi[:, :], 15, None, ALU.bitwise_and), 16, 1, ["ioi"], ["ioj"])
    vop(lambda: V.tensor_scalar(T.oneh[:, :], T.ioj[:, :], 0.0, 256.0, ALU.is_equal, ALU.mult), 16, 1, ["ioj"], ["oneh"])
    vop(lambda: V.memset(T.lk[:, :], 0.0), 2048, .5, (), ["lk%d" % k for k in range(16)])
    for k in range(16):
        vop(lambda k=k: V.tensor_scalar(T.lk[:, 129 * k:128 * k + 128:16], T.bo[:, 0:128:16], K, None, ALU.mult), 8, 1, ["bo"], ["lk%d" % k])
        sop(lambda k=k: S.activation(T.sk[:, 128 * k:128 * k + 128], T.bo[:, :], ACT.Identity, scale=T.oneh[:, k:k + 1]), 128,
            ["bo", "oneh"], ["sk%d" % k])
    for s in range(2):
        vop(lambda s=s: V.memset(win[0][s][:, 0:1536], 0.0), 1536, .5, (), ["wo0%d%d" % (s, l) for l in range(3)])

    vop(lambda: V.tensor_scalar(T.cfh[0:16, :], T.cfn[0:16, :], -1536.0, None, ALU.add), 256, 1, ["cfn"], ["cfh"])
    vop(lambda: V.tensor_scalar(T.cvb[0:16, :], T.cfn[0:16, :], 0.0, 32.0, ALU.min, ALU.mult), 256, 1, ["cfn"], ["cvb"])
    vop(lambda: V.tensor_copy(T.cwb[0:16, :], T.cwn[0:16, :]), 256, 1, ["cwn"], ["cwb"])
    vop(lambda: V.tensor_copy(T.dlb[0:48, :], T.dln[0:48, :]), 256, 1, ["dln"], ["dlb"])
    sbanks = ["pma0", "pma1", "pmb"]
    nb = [0]

    def nbank():
        nb[0] += 1
        return sbanks[nb[0] % 3]

    def qcol(s, l):
        return slice(256 * (3 * s + l), 256 * (3 * s + l) + 256)

    def rows_in(l):
        c = slice(512 * l, 512 * l + 512)
        vop(lambda: V.tensor_scalar(T.fdh[:, c], T.fdn[:, c], -1536.0, None, ALU.add), 512, 1, ["fdn%d" % l], ["fdh%d" % l])
        vop(lambda: V.tensor_scalar(T.fvb[:, c], T.fdn[:, c], 0.0, 32.0, ALU.min, ALU.mult), 512, 1, ["fdn%d" % l], ["fvb%d" % l])
        for s in range(2):
            b = nbank()
            it = []
            for h in range(2):
                e = slice(512 * l + 256 * h, 512 * l + 256 * h + 256)
                it += [(T[b][:, 0:256], T.selk[:, sl(s, h)], T.pwn[:, e], 256, 1), (T[b][:, 0:256], T.selk[:, sl(s, h)], T.fvb[:, e], 256, 1),
                       (T[b][:, 0:256], T["self"][:, sl(s, h)], T.fdh[:, e], 256, 1)]
            mm(it, ["selk%d" % s, "self%d" % s, "pwn%d" % l, "fvb%d" % l, "fdh%d" % l], [b], [b])
            sop(lambda b=b, s=s: S.activation(T.qs[:, qcol(s, l)], T[b][:, 0:256], ACT.Relu, bias=K + 1536.0), 256, [b], ["q%d%d" % (s, l)], [b])
            if l == 0:
                b = nbank()
                c1 = slice(128 * s, 128 * s + 128)
                it = [(T[b][:, 0:256], T.sel8k[0:16, c1], T.cwb[0:16, :], 256, 1), (T[b][:, 0:256], T.sel8k[0:16, c1], T.cvb[0:16, :], 256, 1),
                      (T[b][:, 0:256], T.sel8f[0:16, c1], T.cfh[0:16, :], 256, 1)]
                mm(it, ["sel8k%d" % s, "sel8f%d" % s, "cwb", "cvb", "cfh"], [b], [b])
                sop(lambda b=b, s=s: S.activation(T["inn%d" % s][:, :], T[b][:, 0:256], ACT.Relu, bias=K + 1536.0), 256, [b], ["in%d" % s], [b])

    def delays_in(l):
        for s in range(2):
            b = nbank()
            o = 128 * (3 * s + l)
            it = [(T[b][:, 0:256], T.seld[0:48, o:o + 128], T.dlb[0:48, :], 256, 1), (T[b][:, 0:256], T.im256[:, :], T.ramp[:, :], 256, 1)]
            mm(it, ["seld%d%d" % (s, l), "dlb", "im256", "ramp"], [b], [b])
            sop(lambda b=b, s=s: S.activation(T.dr[:, qcol(s, l)], T[b][:, 0:256], ACT.Identity, bias=-0.25), 256, [b], ["dr%d%d" % (s, l)], [b])

    vop(lambda: V.tensor_copy(T.nxu[:, :], T.nxn[:, :]), 96, 1, ["nxn"], ["nxu"])
    for h in range(2):
        o = 128 * h + 64 * h
        i0 = 256 + 128 * h + 64 * h
        scale(T.selr[:, 128 * h:128 * h + 128], T.sel[:, 256 + 128 * h:384 + 128 * h], 1, 128, ["sel1%d" % h], ["selr%d" % h])
        scale(T.selr[:, o + 16:o + 64], T.sel[:, i0:i0 + 48], 1, 48, ["sel1%d" % h], ["selr%d" % h])
        scale(T.selr[:, o:o + 16], T.sel[:, i0 + 48:i0 + 64], 1, 16, ["sel1%d" % h], ["selr%d" % h])

    def ways_in(l):
        c = slice(512 * l, 512 * l + 512)
        d = slice(32 * l, 32 * l + 32)
        vop(lambda: V.tensor_copy(T.invn[:, c].indirect(T.nxu[:, d]), T.iov[:, :]), 512, 3.8, ["nxu", "iov"], ["invn%d" % l])
        b = nbank()
        mm([(T[b][:, 0:32], T.lk[:, 128 * i:128 * i + 128], T.invn[:, 512 * l + i:512 * l + 512:16], 32, 1) for i in range(16)],
           ["invn%d" % l] + ["lk%d" % k for k in range(16)], [b], [b])
        sop(lambda: S.activation(T.invc[:, d], T[b][:, 0:32], ACT.Identity, scale=1.0 / (16 * K)), 32, [b], ["invc%d" % l], [b])
        for s in range(2):
            it = []
            for h in range(2):
                m = T.selr[:, 128 * h:128 * h + 128] if (s, l) == (1, 2) else T.sel[:, sl(s, h)]
                it.append((T[b][:, 16 * s:16 * s + 16], m, T.invc[:, 32 * l + 16 * h:32 * l + 16 * h + 16], 16, 1))
            mm(it, ["invc%d" % l, "sel%d0" % s, "sel%d1" % s, "selr0", "selr1"], [b], [b])
        vop(lambda: V.tensor_scalar(T.invu[:, d], T[b][:, 0:32], 256.0, None, ALU.add), 32, 1, [b], ["invu%d" % l], [b])

    arr_in = {}
    nblk = [0]

    def level(q, l, s):
        n = str(nlev[0] % 2)
        last = q == 1 and l == 2
        stage[0] = nlev[0] - 1.5
        by_dma = REPDMA == 1 or (REPDMA == 2 and l < 2)
        X, Hb, C = T["px" + n], T["ph" + n], T.pcn
        xb, hb = "px" + n, "ph" + n
        Q, qk = T.qs[:, qcol(s, l)], "q%d%d" % (s, l)
        A, G, R, W = T["aa" + n], T["gg" + n], T["rr" + n], win[q][s]
        Qi, off = T["qi" + n], T["off" + n]
        tcol = slice(256 * (6 * q + 3 * s + l), 256 * (6 * q + 3 * s + l) + 256)
        tk = "tt%d%d%d" % (q, s, l)
        for part in range(2):
            o = Hb[:, 256 * part:256 * part + 256]
            it, r = [], ["selh%d" % s, "bsn%d" % l]
            for h in range(2):
                e = slice(512 * l + 256 * h, 512 * l + 256 * h + 256)
                it.append((o, T.selh[:, sl(s, h)], T.bsn[:, e], 256, 1))
                if q == 0:
                    it.append((o, T.selh[:, sl(s, h)], T.t0n[:, e], 256, 1))
            if q == 0:
                r.append("t0n%d" % l)
            else:
                oc = 256 * (3 * s + l)
                it.append((o, T.ihalf[:, :], T.tt[:, oc:oc + 256], 256, 1))
                r += ["ihalf", "tt0%d%d" % (s, l)]
            if part:
                it.append((o, T.i256[:, :], T.ramp[:, :], 256, 1))
                r += ["i256", "ramp"]
            mm(it, r, [hb + str(part)], [hb])
        if q == 1 and l == 0:
            In, ik = T.inland[:, 256 * s:256 * s + 256], "inland" + n
            op("G", None, 10, (), [ik], kind="w", sem=arr_in[s][1], after=arr_in[s][0])
        else:
            In, ik = T["inn" + n][:, :], "in" + n
        sop(lambda: S.activation(T["edn" + n][:, :], Q, ACT.Exp, bias=C_DN, scale=-EA), 256, [qk], ["edn" + n])
        if l == 0:
            sop(lambda: S.activation(T["ein" + n][:, :], In, ACT.Exp, bias=C_DN, scale=-EA), 256, [ik], ["ein" + n])
        x0, x1 = X[:, 0:256], X[:, 256:512]
        mm([(x0, T.mwin[:, :], T["edn" + n][:, :], 256, 1), (x0, T.ineg[:, :], T["ein" + n][:, :], 256, 1)],
           ["mwin", "ineg", "edn" + n, "ein" + n], [xb + "a"], [xb])
        vop(lambda: V.tensor_tensor(x0, x0, In, ALU.min), 256, 1, [ik, xb + "a"], [xb + "a"], [xb])
        vop(lambda: V.tensor_tensor(Qi[:, :], x0, Q, ALU.max), 256, 1, [qk, xb + "a"], ["qi" + n], [xb])
        vop(lambda: V.tensor_scalar(T["fi" + n][:, :], Qi[:, :], int(K) - 1, None, ALU.bitwise_and), 256, 1, ["qi" + n], ["fi" + n])
        vop(lambda: V.tensor_copy(off[:, :], T["fi" + n][:, :]), 256, 1, ["fi" + n], ["off" + n])
        if not last:
            vop(lambda: V.tensor_tensor(x0, x0, Q, ALU.subtract), 256, 1, [qk, xb + "a"], [xb + "a"], [xb])
            sop(lambda: S.activation(T["dlt" + n][:, :], x0, ACT.Relu), 256, [xb + "a"], ["dlt" + n], [xb])
            if HPE:
                mm([(x1, T.bof[:, :], T["dlt" + n][:, :], 256, 4), (x1, T.inf[:, :], In, 256, 4)], ["bof", "inf", ik, "dlt" + n], [xb + "b"], [xb])
                sop(lambda: S.activation(T["hh" + n][:, :], x1, ACT.Identity, scale=-1.0), 256, [xb + "b"], ["hh" + n], [xb])
            else:
                mm([(x1, T.bof[:, :], T["dlt" + n][:, :], 256, 4)], ["bof", "dlt" + n], [xb + "b"], [xb])
                vop(lambda: V.tensor_tensor(T["hh" + n][:, :], In, x1, ALU.subtract), 256, 1, [ik, xb + "b"], ["hh" + n], [xb])
            sop(lambda: S.activation(T["eh" + n][:, :], T["hh" + n][:, :], ACT.Exp, bias=C_UP, scale=EA), 256, ["hh" + n], ["eh" + n])
            if not by_dma:
                dma(spread(T["hrep" + n], 0, T["hh" + n], 0, l == 2 and s == 1), 262144, ["hh" + n], ["hrep" + n])
        stage[0] = nlev[0]
        nlev[0] += 1
        wk = ["wo%d%d%d" % (q, s, i) for i in range(3)] + ["wf%d%d%d" % (q, s, i) for i in range(3)]
        for i in range(4):
            a, e = 64 * i, 64 * i + 64
            if i % GSTEP:
                continue
            e = a + 64 * GSTEP
            sop(lambda a=a, e=e: S.activation(A[:, 16 * a:16 * e], W[:, :].indirect(off[:, a:e]), ACT.Copy), 16 * (e - a) * GTH,
                wk + ["off" + n], ["aa%s_%d" % (n, j) for j in range(i, i + GSTEP)])
        Y = T["yy" + n]
        NC = len(CHUNKS)
        for ch in range(NC):
            blks = list(range(sum(CHUNKS[:ch]), sum(CHUNKS[:ch + 1])))
            cw = 64 * len(blks)
            e = slice(64 * blks[0], 64 * blks[0] + cw)
            aks = ["aa%s_%d" % (n, j) for j in blks]
            c0 = C[:, e]
            mm([(c0, T.c256[:, :], T.ones[:, e], cw, 1)], ["c256", "ones"], ["cn"], ["pcn"], stop=False)
            for k in range(16):
                gk = G[:, 256 * k + e.start:256 * k + e.stop]
                vop(lambda k=k, gk=gk, e=e: V.tensor_tensor(gk, A[:, 16 * e.start + k:16 * e.stop:16], Hb[:, e], ALU.is_gt), cw, 1,
                    aks + [hb + "0"] + (["tt002", "insend0"] if (q, l, s) == (0, 2, 1) and 16 * ch + k >= RUSH else []),
                    ["gg%s_%d_%d" % (n, k, ch)], [hb])
                mm([(c0, T.lk[:, 128 * k:128 * k + 128], gk, cw, 1)], ["lk%d" % k, "gg%s_%d_%d" % (n, k, ch)], ["cn"], ["pcn"],
                   start=False, stop=k == 15)
            vop(lambda c0=c0, e=e: V.tensor_tensor(c0, c0, Qi[:, e], ALU.is_gt), cw, 1, ["cn", "qi" + n], ["cn"], ["pcn"])
            vop(lambda c0=c0, e=e: V.tensor_tensor(Y[:, e], T.ramp[:, e], c0, ALU.subtract), cw, 1, ["cn", "ramp"], ["yy%s_%d" % (n, ch)], ["pcn"])
            if not last:
                vop(lambda c0=c0, e=e: V.tensor_tensor(T["eup" + n][:, e], c0, Qi[:, e], ALU.mult), cw, 1,
                    ["cn", "qi" + n], ["eup%s_%d" % (n, ch)], ["pcn"])
                sop(lambda e=e: S.activation(T["ed" + n][:, e], T["eup" + n][:, e], ACT.Exp, bias=C_UP, scale=EA), cw,
                    ["eup%s_%d" % (n, ch)], ["ed%s_%d" % (n, ch)])
            for blk in blks:
                par = nblk[0] % 2
                nblk[0] += 1
                ba = "pma%d" % par
                mb = T.mbs[:, 512 * par:512 * par + 512]
                for odd, b in ((1, "pmb"), (0, ba)):
                    it = [(T[b][:, :], T.ident[:, :], A[:, 1024 * blk + odd:1024 * blk + 1024:2], 512, 1)]
                    for kk in range(8):
                        k = 2 * kk + odd
                        it.append((T[b][:, kk:512:8], T.sk[:, 128 * k:128 * k + 128], Y[:, 64 * blk:64 * blk + 64], 64, 1))
                    mm(it, ["aa%s_%d" % (n, blk), "ident", "yy%s_%d" % (n, ch)] + ["sk%d" % k for k in range(16)], [b], [b])
                    if odd:
                        sop(lambda mb=mb: S.activation(mb, T.pmb[:, :], ACT.Copy), 512, ["pmb"], ["mbs%d" % par], ["pmb"])
                vop(lambda ba=ba, mb=mb, blk=blk: V.tensor_tensor_scan(R[:, 512 * blk:512 * blk + 512], T[ba][:, :], mb, -1024.0, ALU.max, ALU.max),
                    512, 1, [ba, "mbs%d" % par], ["rr%s_%d" % (n, blk)], [ba])
        if not last:
            mm([(x0, T.mwin[:, :], T["ed" + n][:, :], 256, 1), (x0, T.ineg[:, :], T["eh" + n][:, :], 256, 1)],
               ["mwin", "ineg", "eh" + n] + ["ed%s_%d" % (n, ch) for ch in range(NC)], [xb + "a"], [xb])
            vop(lambda: V.tensor_tensor(x0, x0, Qi[:, :], ALU.min), 256, 1, ["qi" + n, xb + "a"], [xb + "a"], [xb])
            sop(lambda: S.activation(T["gq" + n][:, :], x0, ACT.Relu), 256, [xb + "a"], ["gq" + n], [xb])
            turn = 2 if (l == 2 and s == 1) else 0
            Rp, H2 = T["rep" + n], T["hrep" + n]
        if not last and by_dma:
            mm([(x1, T.bof[:, :], T["gq" + n][:, :], 256, 4)], ["bof", "gq" + n], [xb + "b"], [xb])
            if l < 2:
                vop(lambda: V.tensor_tensor(H2[:, 0:256], x1, T["hh" + n][:, :], ALU.max), 256, 1, ["hh" + n, xb + "b"], ["hrep" + n], [xb])
            else:
                vop(lambda: V.tensor_tensor(T.outi[:, 0:256], x1, T["hh" + n][:, :], ALU.max), 256, 1, ["hh" + n, xb + "b"], ["outi"], [xb])
                vop(lambda: V.tensor_scalar(T.outj[:, 0:256], T.outi[:, 0:256], 31 * int(K), None, ALU.bitwise_and), 256, 1, ["outi"], ["outj"])
                for h in range(2):
                    p = slice(64 * h, 64 * h + 64)
                    vop(lambda h=h, p=p: V.tensor_tensor(H2[p, 0:256], T.outj[p, 0:256], T.ioe[p, 256 * h:256 * h + 256], ALU.add), 256, 2,
                        ["outj", "ioe"], ["hrep" + n])
            dma(spread(Rp, 0, H2, 0, turn), 262144, ["hrep" + n], ["rep" + n])
        if not last and not by_dma:
            mm([(X[:, 256 * h:256 * h + 256], T.bsum[:, 128 * (turn + h):128 * (turn + h) + 128], T["gq" + n][:, :], 256, 4) for h in range(2)],
               ["bsum%d" % (turn + h) for h in range(2)] + ["gq" + n], [xb + "a", xb + "b"], [xb], apart=True)
            if l < 2:
                vop(lambda: V.tensor_tensor(Rp[:, :], X[:, :], H2[:, :], ALU.max), 512, 1, ["hrep" + n, xb + "a", xb + "b"], ["rep" + n], [xb])
            else:
                vop(lambda: V.tensor_tensor(T.outi[:, :], X[:, :], H2[:, :], ALU.max), 512, 1, ["hrep" + n, xb + "a", xb + "b"], ["outi"], [xb])
                vop(lambda: V.tensor_scalar(T.outj[:, :], T.outi[:, :], 31 * int(K), None, ALU.bitwise_and), 512, 1, ["outi"], ["outj"])
                vop(lambda: V.tensor_tensor(Rp[:, :], T.outj[:, :], T.ioe[:, :], ALU.add), 512, 2, ["outj", "ioe"], ["rep" + n])
        if not last:
            io = 32 * l + 16 * s
            way = Rp[:, :].indirect(T.invu[:, io:io + 16])
            if l < 2:
                sop(lambda: S.activation(T["ein" + n][:, :], way, ACT.Exp, bias=C_DN, scale=-EA), 256 * GTH, ["rep" + n, "invu%d" % l], ["ein" + n])
                sop(lambda: S.activation(T["inn" + n][:, :], way, ACT.Copy), 256 * GTH, ["rep" + n, "invu%d" % l], ["in" + n])
            else:
                c = slice(256 * s, 256 * s + 256)
                sop(lambda: S.activation(T.insend[:, c], way, ACT.Copy), 256 * GTH, ["rep" + n, "invu%d" % l], ["insend" + n])
                d = slice(256 * (1 - s), 256 * (1 - s) + 256)
                arr_in[1 - s] = send(T.inland[:, d], T.insend[:, c], 131072, ["insend" + n])
            if q == 0:
                vop(lambda: V.tensor_tensor(Q, Qi[:, :], T["gq" + n][:, :], ALU.subtract), 256, 2, ["qi" + n, "gq" + n], [qk])
        h1 = Hb[:, 256:512]
        vop(lambda: V.tensor_tensor(h1, h1, R[:, 7:2048:8], ALU.max), 256, 1, [hb + "1"] + ["rr%s_%d" % (n, i) for i in range(4)], [hb + "1"], [hb])
        vop(lambda: V.tensor_tensor(T["vi" + n][:, :], h1, T.dr[:, qcol(s, l)], ALU.add), 256, 1, [hb + "1", "dr%d%d" % (s, l)], ["vi" + n], [hb])
        vop(lambda: V.tensor_scalar(T.tt[:, tcol], T["vi" + n][:, :], 255.0, None, ALU.min), 256, 1, ["vi" + n], [tk])
        if l < 2:
            dma(spread(W, 512 * l, T.tt, tcol.start, False), 131072, [tk], ["wo%d%d%d" % (q, s, l)])
        if q == 0:
            o = 256 * (3 * (1 - s) + l)
            a = send(T.landt[:, o:o + 256], T.tt[:, tcol], 65536, [tk])
            dma(spread(win[1][1 - s], 1536 + 512 * l, T.landt, o, s == 1), 131072, (), ["wf1%d%d" % (1 - s, l)], sem=a[1], after=a[0])
        else:
            for h in range(2):
                pairs = [(T.yt[16 * (2 * j + s):16 * (2 * j + s) + 16, 512 * l + 256 * h:512 * l + 256 * h + 256],
                          T.tt[64 * h + 16 * j:64 * h + 16 * j + 16, tcol]) for j in range(4)]
                dma(pairs, 32768, [tk], (), q="S" if (h == 1 and last and s == 0) else "Y")

    def spread(dst, dcol, src, scol, turn):
        pairs = []
        for h in range(2):
            for hd in range(2):
                dc = slice(dcol + 256 * h, dcol + 256 * h + 256)
                sc = slice(scol, scol + 256)
                if turn:
                    pairs.append((dst[64 * hd + 16:64 * hd + 64, dc], src[64 * h:64 * h + 48, sc]))
                    pairs.append((dst[64 * hd:64 * hd + 16, dc], src[64 * h + 48:64 * h + 64, sc]))
                else:
                    pairs.append((dst[64 * hd:64 * hd + 64, dc], src[64 * h:64 * h + 64, sc]))
        return pairs

    rows_in(0)
    stage[0] = -1.0
    delays_in(0)
    ways_in(0)
    for q in range(2):
        for l in range(3):
            for s in ((0, 1) if q == 0 else (1, 0)):
                for i in range(6):
                    if SETUP[i] == nlev[0]:
                        (rows_in, delays_in, ways_in)[i % 3](1 + i // 3)
                level(q, l, s)
                if q == 0 and l == 1:
                    gop(lambda s=s: g.iota(win[1][s][:, 0:1536], [[0, 1536]], 0, 0, allow_small_or_imprecise_dtypes=True), 1536,
                        ["tt0%d0" % s], ["wo1%d%d" % (s, i) for i in range(3)])
    return ops, nrem[0] * neng


def list_schedule(ops):
    n = len(ops)
    pre = [[] for _ in ops]
    suc = [[] for _ in ops]
    for j, o in enumerate(ops):
        for i in set(o["deps"]) | ({o["after"]} if o["after"] is not None else set()):
            same = ops[i]["eng"] == o["eng"] and ops[i]["lat"] == 0
            w = ops[i]["lat"] + (0.0 if same and o["eng"] == "P" else 40.0 if same else HOP)
            pre[j].append((i, w))
            suc[i].append((j, w))
    tail = [o["lat"] for o in ops]
    best = None
    for t in range(TRIES):
        if t % 2:
            start = greedy(ops, t)[1]
        else:
            left = [len(p) for p in pre]
            key = [(o["key"] + ((i * 7919 + t * 104729) * 2654435761 % 4096) / 4096.0 * 0.02 * t, i) for i, o in enumerate(ops)]
            ready, order = [i for i in range(n) if not left[i]], []
            while ready:
                i = min(ready, key=lambda i: key[i])
                ready.remove(i)
                order.append(i)
                for j, _ in suc[i]:
                    left[j] -= 1
                    if not left[j]:
                        ready.append(j)
            start = place(ops, pre, order, [0.0] * n)
        for _ in range(PASSES):
            back = place(ops, suc, sorted(range(n), key=lambda i: -start[i] - ops[i]["cost"]), tail)
            start = place(ops, pre, sorted(range(n), key=lambda i: -back[i] - ops[i]["cost"]), [0.0] * n)
            end = [start[i] + ops[i]["cost"] + ops[i]["lat"] for i in range(n)]
            if best is None or max(end) < max(best[2]):
                best = (sorted(range(n), key=lambda i: (start[i], i)), start, end)
    kind = [(o["key"], o["w"][:2]) for o in ops]
    kinds = sorted(set(kind))
    rnd = [12345]

    def rand():
        rnd[0] = (rnd[0] * 1103515245 + 12345) % 2147483648
        return rnd[0] / 2147483648.0

    cur = best
    for t in range(ROUNDS):
        mid, wide, size = rand() * 13 - 2, 0.6 + 2 * rand(), 8000 * rand() ** 2
        move = {k: (size * (2 * rand() - 1) if abs(k[0] - mid) < wide and rand() < 0.4 else 0.0) for k in kinds}
        key = [cur[1][i] + move[kind[i]] for i in range(n)]
        for i in range(n):
            for d, _ in pre[i]:
                if key[i] <= key[d]:
                    key[i] = key[d] + 1.0
        start = place(ops, pre, sorted(range(n), key=lambda i: key[i]), [0.0] * n)
        back = place(ops, suc, sorted(range(n), key=lambda i: -start[i] - ops[i]["cost"]), tail)
        start = place(ops, pre, sorted(range(n), key=lambda i: -back[i] - ops[i]["cost"]), [0.0] * n)
        end = [start[i] + ops[i]["cost"] + ops[i]["lat"] for i in range(n)]
        if max(end) < max(cur[2]) + 150:
            cur = (sorted(range(n), key=lambda i: (start[i], i)), start, end)
            if max(end) < max(best[2]):
                best = cur
    return best


def place(ops, pre, order, first):
    start, lines = [0.0] * len(ops), {}
    for i in order:
        c = ops[i]["cost"]
        t = max([first[i]] + [start[d] + ops[d]["cost"] + w for d, w in pre[i]])
        line = lines.setdefault(ops[i]["eng"], [])
        lo, hi = 0, len(line)
        while lo < hi:
            mid = (lo + hi) // 2
            if line[mid][1] <= t:
                lo = mid + 1
            else:
                hi = mid
        while lo < len(line) and line[lo][0] < t + c:
            t = max(t, line[lo][1])
            lo += 1
        line.insert(lo, (t, t + c))
        start[i] = t
    return start


def greedy(ops, seed):
    n = len(ops)
    slack = SLACK * (seed % 4) / 2
    jit = [((i * 7919 + seed * 104729) * 2654435761 % 4096) / 4096.0 * 150.0 * (seed // 4) ** 0.5 for i in range(n)]
    pre = [set(o["deps"]) | ({o["after"]} if o["after"] is not None else set()) for o in ops]
    suc = [[] for _ in ops]
    for i in range(n):
        for d in pre[i]:
            suc[d].append(i)
    hop = HOP
    pr = [0.0] * n
    for i in range(n - 1, -1, -1):
        pr[i] = ops[i]["cost"] + ops[i]["lat"] + hop + max([pr[j] for j in suc[i]] + [0.0])
    left = [len(p) for p in pre]
    rdy = [0.0] * n
    pool = {}
    for i in range(n):
        if left[i] == 0:
            pool.setdefault(ops[i]["eng"], []).append(i)
    free, order, end, start = {}, [], [0.0] * n, [0.0] * n
    for _ in range(n):
        best = None
        for e, lst in pool.items():
            if not lst:
                continue
            t = max(free.get(e, 0.0), min(rdy[i] for i in lst))
            i = max((i for i in lst if rdy[i] <= t + 60.0), key=lambda i: (pr[i] + jit[i], -i))
            i = max((j for j in lst if rdy[j] <= t + 60.0 + slack * ops[i]["cost"]), key=lambda j: (pr[j] + jit[j], -j))
            t = max(t, rdy[i])
            if best is None or t < best[0]:
                best = (t, e, i)
        t, e, i = best
        pool[e].remove(i)
        start[i] = t
        free[e] = t + ops[i]["cost"]
        end[i] = free[e] + ops[i]["lat"]
        order.append(i)
        for j in suc[i]:
            same = ops[j]["eng"] == e and ops[i]["lat"] == 0
            rdy[j] = max(rdy[j], end[i] + (0.0 if same and e == "P" else 40.0 if same else hop))
            left[j] -= 1
            if left[j] == 0:
                pool.setdefault(ops[j]["eng"], []).append(j)
    return order, start, end


def rank_program(g, core, T, topo):
    if T.rank_of(core) is None:
        return
    ops, nsent = build_graph(g, T, topo, core)
    if not ORDER:
        ORDER.append(list_schedule(ops)[0])
    order = ORDER[0]
    queue = {"V": g.vector, "S": g.scalar, "P": g.tensor, "G": g, "Y": g.sync}
    count = {"V": 0, "S": 0, "P": 0, "G": 0}
    done, seen, total, nd = {}, {}, {}, 0

    def wait(e, name, sem, val):
        if seen.get((e, name), 0) < val:
            queue[e].wait_ge(sem, val)
            seen[(e, name)] = val

    for i in order:
        o = ops[i]
        e = o["eng"]
        need = {}
        for d in o["deps"]:
            if ops[d]["eng"] == "P" and e == "P":
                continue
            for name, sem, val in done[d]:
                if need.get(name, (None, 0))[1] < val:
                    need[name] = (sem, val)
        if o["kind"] == "w":
            done[i] = [("a%d" % o["after"], o["sem"][0], o["sem"][1])] + [(k, v[0], v[1]) for k, v in need.items()]
            total["a%d" % o["after"]] = o["sem"]
            continue
        if o["sem"] is not None:
            need["a%d" % o["after"]] = o["sem"]
            total["a%d" % o["after"]] = o["sem"]
        for name in sorted(need):
            wait(e, name, need[name][0], need[name][1])
        if o["kind"] == "d":
            sem = T.sem["d%d" % nd]
            for out, in_ in o["fn"]:
                queue[e].dma_start(out, in_).then_inc(sem, 16)
            done[i] = [("d%d" % nd, sem, 16 * len(o["fn"]))]
            total["d%d" % nd] = (sem, 16 * len(o["fn"]))
            nd += 1
        elif o["kind"] == "r":
            o["fn"]()
            done[i] = []
        else:
            count[e] += 1
            o["fn"]().then_inc(T.sem["e" + e], 1)
            done[i] = [("e" + e, T.sem["e" + e], count[e])]
            total["e" + e] = (T.sem["e" + e], count[e])
    total["sent"] = (T.sem.sent, nsent)
    for name in sorted(total):
        if all(seen.get((e, name), 0) < total[name][1] for e in queue):
            wait("G", name, total[name][0], total[name][1])
